import numpy as np, ml_dtypes
CORES = [2,3,42,43,82,83,122,123]
N = 8
import mx_ref
NC, G = 512, 2
C = np.float32(0.041)
BF = ml_dtypes.bfloat16
def cut(t, i, w=512):
    return t[:, w * i:w * i + w]
def tile(rs):
    return np.stack(rs, axis=2).reshape(128, -1).astype(BF)
def layer(w, X):
    out = []
    for i in range(G):
        for t in range(len(X)):
            p = mx_ref.matmul(mx_ref.quantize(cut(w, len(X) * i + t)), X[t])
            z = p if t == 0 else z + p
        out.append(z)
    return out
def act(Z):
    return [np.maximum(s * z, 0) * C for z in Z for s in (1, -1)]
def setup_inputs(rng):
    def f(*shape):
        return mx_ref.flush((rng.standard_normal(shape, dtype=np.float32) * np.exp2(rng.integers(-2, 3, shape[:-1] + (1,)))).astype(BF))
    return {"xk": f(N, 128, 512), "xq": f(N, 128, 4 * NC), "wk": f(N, 128, G * 512), "wq": f(N, 128, G * 512)}
def setup_inputs_blocks(rng):
    d = setup_inputs(rng)
    for k in ("xk", "xq", "wk", "wq"): d[k] = mx_ref.spread(d[k], rng, 4)
    return d
def setup_inputs_wide(rng):
    d = setup_inputs(rng)
    for k in ("xk", "xq", "wk", "wq"): d[k] = mx_ref.flush((d[k].astype(np.float32) * np.exp2(rng.integers(-5, 6, (N, 1, 1))).astype(np.float32)).astype(BF))
    return d
def reference(xk, xq, wk, wq):
    K = [mx_ref.quantize(tile(act(layer(wk[j], [mx_ref.quantize(xk[j])])))) for j in range(N)]
    y = np.zeros((N, 128, N * NC), np.float32)
    for r in range(N):
        q = mx_ref.quantize(tile(act(layer(wq[r], [mx_ref.quantize(xq[r])]))))
        for j in range(N):
            y[r][:, NC * j:NC * j + NC] = mx_ref.matmul(K[j], q)
    return {"y": y}

@@ -1,0 +1,214 @@
+from concourse.bass import DstId, RemoteDMATransfer
+from concourse.mybir import dt, AluOpType, ActivationFunctionType
+
+N = 8
+C = 0.041
+KW = 128
+NC = 512
+H = NC // 2
+
+SCRATCH = {
+    "xk_t": ("sbuf", [128, 4 * KW], "bfloat16"),
+    "wk_t": ("sbuf", [128, 8 * KW], "bfloat16"),
+    "xq_t": ("sbuf", [128, 4 * NC], "bfloat16"),
+    "wq_t": ("sbuf", [128, 8 * KW], "bfloat16"),
+    "xk_c": ("sbuf", [128, KW], "float8_e4m3fn_x4"), "xk_s": ("sbuf", [128, KW], "uint8"),
+    "wk_c": ("sbuf", [128, 2 * KW], "float8_e4m3fn_x4"), "wk_s": ("sbuf", [128, 2 * KW], "uint8"),
+    "xq_c": ("sbuf", [128, NC], "float8_e4m3fn_x4"), "xq_s": ("sbuf", [128, NC], "uint8"),
+    "wq_c": ("sbuf", [128, 2 * KW], "float8_e4m3fn_x4"), "wq_s": ("sbuf", [128, 2 * KW], "uint8"),
+    "k_t": ("sbuf", [128, 4 * KW], "bfloat16"),
+    "q_t": ("sbuf", [128, 4 * NC], "bfloat16"),
+    "q_c": ("sbuf", [128, NC], "float8_e4m3fn_x4"), "q_s": ("sbuf", [128, NC], "uint8"),
+    "ka_c": ("sbuf", [128, N * KW], "float8_e4m3fn_x4"), "ka_s": ("sbuf", [128, N * KW], "uint8"),
+    "ps": ("psum", [128, 8 * 512], "float32"),
+    "y_t": ("sbuf", [128, N * NC], "float32"),
+}
+SEMAPHORES = (["ld_xk", "ld_wk", "ld_wq", "ld_xq0", "ld_xq1",
+               "qxk", "qwk0", "qwk1", "zk0", "zk1", "kact", "kq",
+               "qwq", "qxq0", "qxq1", "zq00", "zq10", "zq01", "zq11", "qact0", "qact1", "qq0", "qq1",
+               "my0a", "my0b", "st_sy", "st_sc", "fwd", "sent"]
+              + ["my%d" % u for u in range(1, N)] + ["cp%d" % u for u in range(N)] + ["arr%d" % j for j in range(N)])
+
+
+def _count(mask):
+    return sum((mask >> b) & 1 for b in range(16))
+
+
+def rank_program(g, core, T, topo):
+    rank = T.rank_of(core)
+    if rank is None:
+        return
+    S = T.sem
+    V, A, PE, SY = g.vector, g.scalar, g.tensor, g.sync
+    MAX, MUL = AluOpType.max, AluOpType.mult
+    RELU, COPY = ActivationFunctionType.Relu, ActivationFunctionType.Copy
+
+    cores = list(T.cores)
+    chips = []
+    for c in cores:
+        if topo.chip(c) not in chips:
+            chips.append(topo.chip(c))
+    members = {ch: [c for c in cores if topo.chip(c) == ch] for ch in chips}
+    nch = len(chips)
+    nf = nch - 1
+
+    def near(a, b):
+        return topo.same_plane(a, b) or topo.mates(a, b)
+
+    def send_order(ch):
+        return sorted([x for x in chips if x != ch],
+                      key=lambda x: (0 if near(ch, x) else 1, (chips.index(x) - chips.index(ch)) % nch))
+
+    def recv_order(ch):
+        return sorted([x for x in chips if x != ch],
+                      key=lambda x: (0 if near(ch, x) else 1, (chips.index(ch) - chips.index(x)) % nch))
+
+    def plan(c):
+        ch = topo.chip(c)
+        p = members[ch].index(c)
+        tw = members[ch][1 - p]
+        far = [(members[x][p], 2 + recv_order(x).index(ch)) for x in send_order(ch)]
+        m_on = topo.mask(c, tw)
+        m_far = m_on
+        for d, _ in far:
+            m_far &= topo.mask(c, d)
+        m_tw = (m_on & ~m_far) or m_on
+        return tw, far, m_far, m_tw, m_on
+
+    me = topo.chip(core)
+    pos = members[me].index(core)
+    twin, far, m_far, m_tw, m_on = plan(core)
+
+    def dst_id(c):
+        rid, pid, _ = topo.addr(c)
+        return DstId(rid=rid, pnc=pid)
+
+    def codes(a, n=1):
+        return T.ka_c[:, KW * a:KW * (a + n)].bitcast(dt.uint8)
+
+    def plane(a, n=1):
+        return T.ka_s[:, KW * a:KW * (a + n)]
+
+    src_core = [core, twin] + [members[x][pos] for x in recv_order(me)] + [members[x][1 - pos] for x in recv_order(me)]
+    src_of = [T.rank_of(c) for c in src_core]
+    arrive = {1: (S["arr%d" % src_of[1]], 2 * _count(plan(twin)[3]))}
+    for s in range(2, 2 + nf):
+        arrive[s] = (S["arr%d" % src_of[s]], 2 * _count(plan(src_core[s])[2]))
+    for s in range(2 + nf, N):
+        arrive[s] = (S.fwd, 2 * _count(plan(twin)[4]))
+
+    def bank(b, n=NC):
+        return T.ps[:, 512 * b:512 * b + n]
+
+    SY.dma_start(T.xk_t[:], T.xk[:]).then_inc(S.ld_xk, 16)
+    A.dma_start(T.wk_t[:], T.wk[:]).then_inc(S.ld_wk, 16)
+    A.dma_start(T.wq_t[:], T.wq[:]).then_inc(S.ld_wq, 16)
+    SY.dma_start(T.xq_t[:, 0:4 * H], T.xq[:, 0:4 * H]).then_inc(S.ld_xq0, 16)
+    SY.dma_start(T.xq_t[:, 4 * H:8 * H], T.xq[:, 4 * H:8 * H]).then_inc(S.ld_xq1, 16)
+
+    V.wait_ge(S.ld_xk, 16)
+    V.quantize_mx(T.xk_c[:], T.xk_s[:], T.xk_t[:]).then_inc(S.qxk, 1)
+    V.wait_ge(S.ld_wk, 16)
+    V.quantize_mx(T.wk_c[:, 0:KW], T.wk_s[:, 0:KW], T.wk_t[:, 0:4 * KW]).then_inc(S.qwk0, 1)
+    V.quantize_mx(T.wk_c[:, KW:2 * KW], T.wk_s[:, KW:2 * KW], T.wk_t[:, 4 * KW:8 * KW]).then_inc(S.qwk1, 1)
+    PE.wait_ge(S.qxk, 1)
+    PE.wait_ge(S.qwk0, 1)
+    PE.matmul_mx(bank(0, KW), T.wk_c[:, 0:KW], T.wk_s[:, 0:KW], T.xk_c[:], T.xk_s[:], True, True).then_inc(S.zk0, 1)
+    PE.wait_ge(S.qwk1, 1)
+    PE.matmul_mx(bank(1, KW), T.wk_c[:, KW:2 * KW], T.wk_s[:, KW:2 * KW], T.xk_c[:], T.xk_s[:], True, True).then_inc(S.zk1, 1)
+    A.wait_ge(S.zk0, 1)
+    A.activation(T.k_t[:, 0:4 * KW:4], bank(0, KW), RELU, scale=C).then_inc(S.kact, 1)
+    A.activation(T.k_t[:, 1:4 * KW:4], bank(0, KW), RELU, scale=-C).then_inc(S.kact, 1)
+    V.wait_ge(S.zk1, 1)
+    V.tensor_scalar(T.k_t[:, 2:4 * KW:4], bank(1, KW), 0.0, C, MAX, MUL).then_inc(S.kact, 1)
+    V.tensor_scalar(T.k_t[:, 3:4 * KW:4], bank(1, KW), -C, 0.0, MUL, MAX).then_inc(S.kact, 1)
+    V.wait_ge(S.kact, 4)
+    V.quantize_mx(T.ka_c[:, 0:KW], T.ka_s[:, 0:KW], T.k_t[:]).then_inc(S.kq, 1)
+
+    my_arr = S["arr%d" % rank]
+    sent = 0
+    g.wait_ge(S.kq, 1)
+    for view in (codes, plane):
+        g.remote_dma_fused([RemoteDMATransfer(dst_ids=[dst_id(c) for c, _ in far], dma_engine_mask=m_far,
+                                              remote_sem=my_arr, srcs=[view(0)], dsts=[view(s) for _, s in far])],
+                           local_sem=S.sent)
+        sent += _count(m_far)
+    for view in (codes, plane):
+        g.remote_dma_fused([RemoteDMATransfer(dst_ids=[dst_id(twin)], dma_engine_mask=m_tw, remote_sem=my_arr,
+                                              srcs=[view(0)], dsts=[view(1)])], local_sem=S.sent)
+        sent += _count(m_tw)
+
+    for s in range(2, 2 + nf):
+        g.wait_ge(*arrive[s])
+    for view in (codes, plane):
+        g.remote_dma_fused([RemoteDMATransfer(dst_ids=[dst_id(twin)], dma_engine_mask=m_on, remote_sem=S.fwd,
+                                              srcs=[view(2, nf)], dsts=[view(2 + nf, nf)])], local_sem=S.sent)
+        sent += _count(m_on)
+    g.wait_ge(S.sent, sent)
+
+    V.wait_ge(S.ld_wq, 16)
+    V.quantize_mx(T.wq_c[:], T.wq_s[:], T.wq_t[:]).then_inc(S.qwq, 1)
+    PE.wait_ge(S.qwq, 1)
+    for h in range(2):
+        cw = slice(H * h, H * h + H)
+        V.wait_ge(S["ld_xq%d" % h], 16)
+        V.quantize_mx(T.xq_c[:, cw], T.xq_s[:, cw], T.xq_t[:, 4 * H * h:4 * H * (h + 1)]).then_inc(S["qxq%d" % h], 1)
+        PE.wait_ge(S["qxq%d" % h], 1)
+        for i in range(2):
+            PE.matmul_mx(bank(2 + 2 * h + i, H), T.wq_c[:, KW * i:KW * (i + 1)], T.wq_s[:, KW * i:KW * (i + 1)],
+                         T.xq_c[:, cw], T.xq_s[:, cw], True, True).then_inc(S["zq%d%d" % (i, h)], 1)
+    for h in range(2):
+        cw = slice(H * h, H * h + H)
+        lo, hi = 4 * H * h, 4 * H * (h + 1)
+        act = S["qact%d" % h]
+        V.wait_ge(S["zq0%d" % h], 1)
+        V.tensor_scalar(T.q_t[:, lo + 0:hi:4], bank(2 + 2 * h, H), 0.0, C, MAX, MUL).then_inc(act, 1)
+        V.tensor_scalar(T.q_t[:, lo + 1:hi:4], bank(2 + 2 * h, H), -C, 0.0, MUL, MAX).then_inc(act, 1)
+        A.wait_ge(S["zq1%d" % h], 1)
+        A.activation(T.q_t[:, lo + 2:hi:4], bank(3 + 2 * h, H), RELU, scale=C).then_inc(act, 1)
+        A.activation(T.q_t[:, lo + 3:hi:4], bank(3 + 2 * h, H), RELU, scale=-C).then_inc(act, 1)
+        V.wait_ge(act, 4)
+        V.quantize_mx(T.q_c[:, cw], T.q_s[:, cw], T.q_t[:, lo:hi]).then_inc(S["qq%d" % h], 1)
+
+    def ycols(s, a=0, n=NC):
+        j = src_of[s]
+        return slice(NC * j + a, NC * j + a + n)
+
+    PE.wait_ge(S.kq, 1)
+    PE.wait_ge(S.qq0, 1)
+    PE.matmul_mx(bank(6, H), T.ka_c[:, 0:KW], T.ka_s[:, 0:KW], T.q_c[:, 0:H], T.q_s[:, 0:H], True, True).then_inc(S.my0a, 1)
+    PE.wait_ge(S.qq1, 1)
+    PE.matmul_mx(bank(7, H), T.ka_c[:, 0:KW], T.ka_s[:, 0:KW], T.q_c[:, H:NC], T.q_s[:, H:NC], True, True).then_inc(S.my0b, 1)
+    A.wait_ge(S.my0a, 1)
+    A.activation(T.y_t[:, ycols(0, 0, H)], bank(6, H), COPY).then_inc(S.cp0, 1)
+    V.wait_ge(S.my0b, 1)
+    V.tensor_copy(T.y_t[:, ycols(0, H, H)], bank(7, H)).then_inc(S.cp0, 1)
+    SY.wait_ge(S.cp0, 2)
+    SY.dma_start(T.y[:, ycols(0)], T.y_t[:, ycols(0)]).then_inc(S.st_sy, 16)
+    n_sy, n_sc = 1, 0
+
+    PE.wait_ge(S.kact, 4)
+    PE.wait_ge(S.qact0, 4)
+    PE.wait_ge(S.qact1, 4)
+    for s in range(1, N):
+        b = s - 1
+        PE.wait_ge(*arrive[s])
+        if b >= 6:
+            PE.wait_ge(S.cp0, 2)
+        PE.matmul_mx(bank(b), T.ka_c[:, KW * s:KW * (s + 1)], T.ka_s[:, KW * s:KW * (s + 1)], T.q_c[:], T.q_s[:],
+                     True, True).then_inc(S["my%d" % s], 1)
+        cp = S["cp%d" % s]
+        if s % 2 == 1:
+            A.wait_ge(S["my%d" % s], 1)
+            A.activation(T.y_t[:, ycols(s)], bank(b), COPY).then_inc(cp, 1)
+            A.wait_ge(cp, 1)
+            A.dma_start(T.y[:, ycols(s)], T.y_t[:, ycols(s)]).then_inc(S.st_sc, 16)
+            n_sc += 1
+        else:
+            V.wait_ge(S["my%d" % s], 1)
+            V.tensor_copy(T.y_t[:, ycols(s)], bank(b)).then_inc(cp, 1)
+            SY.wait_ge(cp, 1)
+            SY.dma_start(T.y[:, ycols(s)], T.y_t[:, ycols(s)]).then_inc(S.st_sy, 16)
+            n_sy += 1
+    SY.wait_ge(S.st_sy, 16 * n_sy)
+    A.wait_ge(S.st_sc, 16 * n_sc)

@@ -26,8 +26,9 @@ SCRATCH = {
 SEMAPHORES = (["ld_xk", "ld_wk", "ld_wq", "ld_xq0", "ld_xq1",
                "qxk", "qwk0", "qwk1", "zk0", "zk1", "kact", "kq",
                "qwq", "qxq0", "qxq1", "zq00", "zq10", "zq01", "zq11", "qact0", "qact1", "qq0", "qq1",
-               "my0a", "my0b", "st_sy", "st_sc", "fwd", "sent"]
-              + ["my%d" % u for u in range(1, N)] + ["cp%d" % u for u in range(N)] + ["arr%d" % j for j in range(N)])
+               "my0a", "my0b", "st_sy", "st_sc", "sent", "fwp", "myLa", "myLb", "cpL"]
+              + ["my%d" % u for u in range(1, N)] + ["cp%d" % u for u in range(N)]
+              + ["arrp%d" % j for j in range(N)] + ["arrc%d" % j for j in range(N)] + ["fwc%d" % j for j in range(N)])
 
 
 def _count(mask):
@@ -89,13 +90,18 @@ def rank_program(g, core, T, topo):
     def plane(a, n=1):
         return T.ka_s[:, KW * a:KW * (a + n)]
 
+    def fwd_mask(c, s):
+        return plan(c)[4] if s == 1 + nf else plan(c)[3]
+
     src_core = [core, twin] + [members[x][pos] for x in recv_order(me)] + [members[x][1 - pos] for x in recv_order(me)]
     src_of = [T.rank_of(c) for c in src_core]
-    arrive = {1: (S["arr%d" % src_of[1]], 2 * _count(plan(twin)[3]))}
+    e_tw = _count(plan(twin)[3])
+    arrive = {1: [(S["arrp%d" % src_of[1]], e_tw), (S["arrc%d" % src_of[1]], e_tw)]}
     for s in range(2, 2 + nf):
-        arrive[s] = (S["arr%d" % src_of[s]], 2 * _count(plan(src_core[s])[2]))
+        e = _count(plan(src_core[s])[2])
+        arrive[s] = [(S["arrp%d" % src_of[s]], e), (S["arrc%d" % src_of[s]], e)]
     for s in range(2 + nf, N):
-        arrive[s] = (S.fwd, 2 * _count(plan(twin)[4]))
+        arrive[s] = [(S.fwp, e_tw), (S["fwc%d" % s], _count(fwd_mask(twin, s - nf)))]
 
     def bank(b, n=NC):
         return T.ps[:, 512 * b:512 * b + n]
@@ -125,26 +131,27 @@ def rank_program(g, core, T, topo):
     V.wait_ge(S.kact, 4)
     V.quantize_mx(T.ka_c[:, 0:KW], T.ka_s[:, 0:KW], T.k_t[:]).then_inc(S.kq, 1)
 
-    my_arr = S["arr%d" % rank]
-    sent = 0
-    g.wait_ge(S.kq, 1)
-    for view in (codes, plane):
-        g.remote_dma_fused([RemoteDMATransfer(dst_ids=[dst_id(c) for c, _ in far], dma_engine_mask=m_far,
-                                              remote_sem=my_arr, srcs=[view(0)], dsts=[view(s) for _, s in far])],
-                           local_sem=S.sent)
-        sent += _count(m_far)
-    for view in (codes, plane):
-        g.remote_dma_fused([RemoteDMATransfer(dst_ids=[dst_id(twin)], dma_engine_mask=m_tw, remote_sem=my_arr,
-                                              srcs=[view(0)], dsts=[view(1)])], local_sem=S.sent)
-        sent += _count(m_tw)
+    sent = [0]
 
+    def send(view, a, n, dests, mask, sem):
+        g.remote_dma_fused([RemoteDMATransfer(dst_ids=[dst_id(c) for c, _ in dests], dma_engine_mask=mask,
+                                              remote_sem=sem, srcs=[view(a, n)], dsts=[view(s, n) for _, s in dests])],
+                           local_sem=S.sent)
+        sent[0] += _count(mask)
+
+    my_p, my_c = S["arrp%d" % rank], S["arrc%d" % rank]
+    g.wait_ge(S.kq, 1)
+    send(plane, 0, 1, far, m_far, my_p)
+    send(codes, 0, 1, far, m_far, my_c)
+    send(plane, 0, 1, [(twin, 1)], m_tw, my_p)
+    send(codes, 0, 1, [(twin, 1)], m_tw, my_c)
     for s in range(2, 2 + nf):
-        g.wait_ge(*arrive[s])
-    for view in (codes, plane):
-        g.remote_dma_fused([RemoteDMATransfer(dst_ids=[dst_id(twin)], dma_engine_mask=m_on, remote_sem=S.fwd,
-                                              srcs=[view(2, nf)], dsts=[view(2 + nf, nf)])], local_sem=S.sent)
-        sent += _count(m_on)
-    g.wait_ge(S.sent, sent)
+        g.wait_ge(*arrive[s][0])
+    send(plane, 2, nf, [(twin, 2 + nf)], m_tw, S.fwp)
+    for s in range(2, 2 + nf):
+        g.wait_ge(*arrive[s][1])
+        send(codes, s, 1, [(twin, s + nf)], fwd_mask(core, s), S["fwc%d" % (s + nf)])
+    g.wait_ge(S.sent, sent[0])
 
     V.wait_ge(S.ld_wq, 16)
     V.quantize_mx(T.wq_c[:], T.wq_s[:], T.wq_t[:]).then_inc(S.qwq, 1)
@@ -190,15 +197,28 @@ def rank_program(g, core, T, topo):
     PE.wait_ge(S.kact, 4)
     PE.wait_ge(S.qact0, 4)
     PE.wait_ge(S.qact1, 4)
-    for s in range(1, N):
-        b = s - 1
-        PE.wait_ge(*arrive[s])
+    order = list(range(1, N))
+    for b, s in enumerate(order):
+        for w in arrive[s]:
+            PE.wait_ge(*w)
         if b >= 6:
             PE.wait_ge(S.cp0, 2)
+        if b == len(order) - 1:
+            for h, sem in enumerate((S.myLa, S.myLb)):
+                PE.matmul_mx(bank(b + h, H), T.ka_c[:, KW * s:KW * (s + 1)], T.ka_s[:, KW * s:KW * (s + 1)],
+                             T.q_c[:, H * h:H * h + H], T.q_s[:, H * h:H * h + H], True, True).then_inc(sem, 1)
+            V.wait_ge(S.myLa, 1)
+            V.tensor_copy(T.y_t[:, ycols(s, 0, H)], bank(b, H)).then_inc(S.cpL, 1)
+            A.wait_ge(S.myLb, 1)
+            A.activation(T.y_t[:, ycols(s, H, H)], bank(b + 1, H), COPY).then_inc(S.cpL, 1)
+            A.wait_ge(S.cpL, 2)
+            A.dma_start(T.y[:, ycols(s)], T.y_t[:, ycols(s)]).then_inc(S.st_sc, 16)
+            n_sc += 1
+            break
         PE.matmul_mx(bank(b), T.ka_c[:, KW * s:KW * (s + 1)], T.ka_s[:, KW * s:KW * (s + 1)], T.q_c[:], T.q_s[:],
                      True, True).then_inc(S["my%d" % s], 1)
         cp = S["cp%d" % s]
-        if s % 2 == 1:
+        if b % 2 == 0:
             A.wait_ge(S["my%d" % s], 1)
             A.activation(T.y_t[:, ycols(s)], bank(b), COPY).then_inc(cp, 1)
             A.wait_ge(cp, 1)

@@ -6,6 +6,8 @@ C = 0.041
 KW = 128
 NC = 512
 H = NC // 2
+PIECES = [(0, 256), (256, 128), (384, 128)]
+NP = len(PIECES)
 
 SCRATCH = {
     "xk_t": ("sbuf", [128, 4 * KW], "bfloat16"),
@@ -23,12 +25,14 @@ SCRATCH = {
     "ps": ("psum", [128, 8 * 512], "float32"),
     "y_t": ("sbuf", [128, N * NC], "float32"),
 }
-SEMAPHORES = (["ld_xk", "ld_wk", "ld_wq", "ld_xq0", "ld_xq1",
-               "qxk", "qwk0", "qwk1", "zk0", "zk1", "kact", "kq",
-               "qwq", "qxq0", "qxq1", "zq00", "zq10", "zq01", "zq11", "qact0", "qact1", "qq0", "qq1",
-               "my0a", "my0b", "st_sy", "st_sc", "sent", "fwp", "myLa", "myLb", "cpL"]
-              + ["my%d" % u for u in range(1, N)] + ["cp%d" % u for u in range(N)]
-              + ["arrp%d" % j for j in range(N)] + ["arrc%d" % j for j in range(N)] + ["fwc%d" % j for j in range(N)])
+SEMAPHORES = (["ld_xk", "ld_wk", "ld_wq0", "ld_wq1", "qxk", "qwk0", "qwk1", "zk0", "zk1", "kact", "kq", "qwq0", "qwq1",
+               "st_sy", "st_sc", "sent", "fwp"]
+              + ["ld_xq%d" % p for p in range(NP)] + ["qxq%d" % p for p in range(NP)]
+              + ["zq%d%d" % (i, p) for i in range(2) for p in range(NP)]
+              + ["qact%d" % p for p in range(NP)] + ["qq%d" % p for p in range(NP)]
+              + ["mj%d" % u for u in range(11)] + ["cj%d" % u for u in range(11)]
+              + ["arrp%d" % j for j in range(N)] + ["arrc%d" % j for j in range(N)] + ["fwc%d" % j for j in range(N)]
+              + ["hp%d" % j for j in range(N)] + ["hc%d" % j for j in range(N)])
 
 
 def _count(mask):
@@ -36,9 +40,6 @@ def _count(mask):
 
 
 def rank_program(g, core, T, topo):
-    rank = T.rank_of(core)
-    if rank is None:
-        return
     S = T.sem
     V, A, PE, SY = g.vector, g.scalar, g.tensor, g.sync
     MAX, MUL = AluOpType.max, AluOpType.mult
@@ -51,34 +52,55 @@ def rank_program(g, core, T, topo):
             chips.append(topo.chip(c))
     members = {ch: [c for c in cores if topo.chip(c) == ch] for ch in chips}
     nch = len(chips)
-    nf = nch - 1
 
-    def near(a, b):
-        return topo.same_plane(a, b) or topo.mates(a, b)
+    def by_helper(ch):
+        return [x for x in chips if x != ch and topo.same_plane(ch, x)]
+
+    def by_rank(ch):
+        return [x for x in chips if x != ch and not topo.same_plane(ch, x)]
 
     def send_order(ch):
-        return sorted([x for x in chips if x != ch],
-                      key=lambda x: (0 if near(ch, x) else 1, (chips.index(x) - chips.index(ch)) % nch))
+        return sorted(by_rank(ch), key=lambda x: (chips.index(x) - chips.index(ch)) % nch)
 
     def recv_order(ch):
-        return sorted([x for x in chips if x != ch],
-                      key=lambda x: (0 if near(ch, x) else 1, (chips.index(ch) - chips.index(x)) % nch))
+        return sorted(by_rank(ch), key=lambda x: (chips.index(ch) - chips.index(x)) % nch)
+
+    nf = len(by_rank(chips[0]))
+    hs = 2 + 2 * nf
+
+    def helper_dests(c):
+        ch = topo.chip(c)
+        p = members[ch].index(c)
+        out = []
+        for x in by_helper(ch):
+            out += [(members[x][p], hs), (members[x][1 - p], hs + 1)]
+        return out
+
+    def helper(c):
+        ch = topo.chip(c)
+        cand = [h for h in range(topo.CHIPS * topo.CORES_PER_CHIP)
+                if topo.chip(h) == ch and h not in cores and topo.die(h) != topo.die(c)
+                and all(topo.may_write(h, d) for d, _ in helper_dests(c))]
+        return cand[members[ch].index(c)]
 
     def plan(c):
         ch = topo.chip(c)
         p = members[ch].index(c)
         tw = members[ch][1 - p]
         far = [(members[x][p], 2 + recv_order(x).index(ch)) for x in send_order(ch)]
-        m_on = topo.mask(c, tw)
+        m_on = topo.mask(c, tw) & topo.mask(c, helper(c))
         m_far = m_on
         for d, _ in far:
             m_far &= topo.mask(c, d)
         m_tw = (m_on & ~m_far) or m_on
         return tw, far, m_far, m_tw, m_on
 
-    me = topo.chip(core)
-    pos = members[me].index(core)
-    twin, far, m_far, m_tw, m_on = plan(core)
+    def helper_mask(c):
+        h = helper(c)
+        m = topo.mask(h, c)
+        for d, _ in helper_dests(c):
+            m &= topo.mask(h, d)
+        return m
 
     def dst_id(c):
         rid, pid, _ = topo.addr(c)
@@ -90,27 +112,61 @@ def rank_program(g, core, T, topo):
     def plane(a, n=1):
         return T.ka_s[:, KW * a:KW * (a + n)]
 
+    sent = [0]
+
+    def send(view, a, n, dests, mask, sem):
+        g.remote_dma_fused([RemoteDMATransfer(dst_ids=[dst_id(c) for c, _ in dests], dma_engine_mask=mask,
+                                              remote_sem=sem, srcs=[view(a, n)], dsts=[view(s, n) for _, s in dests])],
+                           local_sem=S.sent)
+        sent[0] += _count(mask)
+
+    rank = T.rank_of(core)
+    if rank is None:
+        for c in cores:
+            if helper(c) == core:
+                r = T.rank_of(c)
+                e = _count(plan(c)[3])
+                g.wait_ge(S["arrp%d" % r], e)
+                send(plane, 0, 1, helper_dests(c), helper_mask(c), S["hp%d" % r])
+                g.wait_ge(S["arrc%d" % r], e)
+                send(codes, 0, 1, helper_dests(c), helper_mask(c), S["hc%d" % r])
+                g.wait_ge(S.sent, sent[0])
+        return
+
+    me = topo.chip(core)
+    pos = members[me].index(core)
+    twin, far, m_far, m_tw, m_on = plan(core)
+
     def fwd_mask(c, s):
         return plan(c)[4] if s == 1 + nf else plan(c)[3]
 
-    src_core = [core, twin] + [members[x][pos] for x in recv_order(me)] + [members[x][1 - pos] for x in recv_order(me)]
+    hx = by_helper(me)[0]
+    src_core = ([core, twin] + [members[x][pos] for x in recv_order(me)] + [members[x][1 - pos] for x in recv_order(me)]
+                + [members[hx][pos], members[hx][1 - pos]])
     src_of = [T.rank_of(c) for c in src_core]
     e_tw = _count(plan(twin)[3])
-    arrive = {1: [(S["arrp%d" % src_of[1]], e_tw), (S["arrc%d" % src_of[1]], e_tw)]}
+    arrive = {0: [(S.kq, 1)], 1: [(S["arrp%d" % src_of[1]], e_tw), (S["arrc%d" % src_of[1]], e_tw)]}
     for s in range(2, 2 + nf):
         e = _count(plan(src_core[s])[2])
         arrive[s] = [(S["arrp%d" % src_of[s]], e), (S["arrc%d" % src_of[s]], e)]
-    for s in range(2 + nf, N):
+    for s in range(2 + nf, hs):
         arrive[s] = [(S.fwp, e_tw), (S["fwc%d" % s], _count(fwd_mask(twin, s - nf)))]
+    for s in range(hs, N):
+        e = _count(helper_mask(src_core[s]))
+        arrive[s] = [(S["hp%d" % src_of[s]], e), (S["hc%d" % src_of[s]], e)]
 
     def bank(b, n=NC):
         return T.ps[:, 512 * b:512 * b + n]
 
+    def wtile(c, s, i):
+        return c[:, KW * i:KW * (i + 1)], s[:, KW * i:KW * (i + 1)]
+
     SY.dma_start(T.xk_t[:], T.xk[:]).then_inc(S.ld_xk, 16)
     A.dma_start(T.wk_t[:], T.wk[:]).then_inc(S.ld_wk, 16)
-    A.dma_start(T.wq_t[:], T.wq[:]).then_inc(S.ld_wq, 16)
-    SY.dma_start(T.xq_t[:, 0:4 * H], T.xq[:, 0:4 * H]).then_inc(S.ld_xq0, 16)
-    SY.dma_start(T.xq_t[:, 4 * H:8 * H], T.xq[:, 4 * H:8 * H]).then_inc(S.ld_xq1, 16)
+    for i in range(2):
+        A.dma_start(T.wq_t[:, 4 * KW * i:4 * KW * (i + 1)], T.wq[:, 4 * KW * i:4 * KW * (i + 1)]).then_inc(S["ld_wq%d" % i], 16)
+    for p, (a, n) in enumerate(PIECES):
+        SY.dma_start(T.xq_t[:, 4 * a:4 * (a + n)], T.xq[:, 4 * a:4 * (a + n)]).then_inc(S["ld_xq%d" % p], 16)
 
     V.wait_ge(S.ld_xk, 16)
     V.quantize_mx(T.xk_c[:], T.xk_s[:], T.xk_t[:]).then_inc(S.qxk, 1)
@@ -131,20 +187,13 @@ def rank_program(g, core, T, topo):
     V.wait_ge(S.kact, 4)
     V.quantize_mx(T.ka_c[:, 0:KW], T.ka_s[:, 0:KW], T.k_t[:]).then_inc(S.kq, 1)
 
-    sent = [0]
-
-    def send(view, a, n, dests, mask, sem):
-        g.remote_dma_fused([RemoteDMATransfer(dst_ids=[dst_id(c) for c, _ in dests], dma_engine_mask=mask,
-                                              remote_sem=sem, srcs=[view(a, n)], dsts=[view(s, n) for _, s in dests])],
-                           local_sem=S.sent)
-        sent[0] += _count(mask)
-
     my_p, my_c = S["arrp%d" % rank], S["arrc%d" % rank]
+    on_chip = [(helper(core), 0), (twin, 1)]
     g.wait_ge(S.kq, 1)
     send(plane, 0, 1, far, m_far, my_p)
     send(codes, 0, 1, far, m_far, my_c)
-    send(plane, 0, 1, [(twin, 1)], m_tw, my_p)
-    send(codes, 0, 1, [(twin, 1)], m_tw, my_c)
+    send(plane, 0, 1, on_chip, m_tw, my_p)
+    send(codes, 0, 1, on_chip, m_tw, my_c)
     for s in range(2, 2 + nf):
         g.wait_ge(*arrive[s][0])
     send(plane, 2, nf, [(twin, 2 + nf)], m_tw, S.fwp)
@@ -153,82 +202,77 @@ def rank_program(g, core, T, topo):
         send(codes, s, 1, [(twin, s + nf)], fwd_mask(core, s), S["fwc%d" % (s + nf)])
     g.wait_ge(S.sent, sent[0])
 
-    V.wait_ge(S.ld_wq, 16)
-    V.quantize_mx(T.wq_c[:], T.wq_s[:], T.wq_t[:]).then_inc(S.qwq, 1)
-    PE.wait_ge(S.qwq, 1)
-    for h in range(2):
-        cw = slice(H * h, H * h + H)
-        V.wait_ge(S["ld_xq%d" % h], 16)
-        V.quantize_mx(T.xq_c[:, cw], T.xq_s[:, cw], T.xq_t[:, 4 * H * h:4 * H * (h + 1)]).then_inc(S["qxq%d" % h], 1)
-        PE.wait_ge(S["qxq%d" % h], 1)
+    def quant_wq(i):
+        V.wait_ge(S["ld_wq%d" % i], 16)
+        V.quantize_mx(T.wq_c[:, KW * i:KW * (i + 1)], T.wq_s[:, KW * i:KW * (i + 1)],
+                      T.wq_t[:, 4 * KW * i:4 * KW * (i + 1)]).then_inc(S["qwq%d" % i], 1)
+
+    def quant_xq(p):
+        a, n = PIECES[p]
+        V.wait_ge(S["ld_xq%d" % p], 16)
+        V.quantize_mx(T.xq_c[:, a:a + n], T.xq_s[:, a:a + n], T.xq_t[:, 4 * a:4 * (a + n)]).then_inc(S["qxq%d" % p], 1)
+
+    def signs_v(p):
+        a, n = PIECES[p]
+        V.wait_ge(S["zq0%d" % p], 1)
+        V.tensor_scalar(T.q_t[:, 4 * a + 0:4 * (a + n):4], bank(2 + 2 * p, n), 0.0, C, MAX, MUL).then_inc(S["qact%d" % p], 1)
+        V.tensor_scalar(T.q_t[:, 4 * a + 1:4 * (a + n):4], bank(2 + 2 * p, n), -C, 0.0, MUL, MAX).then_inc(S["qact%d" % p], 1)
+
+    def quant_q(p):
+        a, n = PIECES[p]
+        V.wait_ge(S["qact%d" % p], 4)
+        V.quantize_mx(T.q_c[:, a:a + n], T.q_s[:, a:a + n], T.q_t[:, 4 * a:4 * (a + n)]).then_inc(S["qq%d" % p], 1)
+
+    quant_wq(0)
+    quant_xq(0)
+    quant_wq(1)
+    quant_xq(1)
+    signs_v(0)
+    quant_xq(2)
+    quant_q(0)
+    signs_v(1)
+    quant_q(1)
+    signs_v(2)
+    quant_q(2)
+    for p, (a, n) in enumerate(PIECES):
+        PE.wait_ge(S["qxq%d" % p], 1)
         for i in range(2):
-            PE.matmul_mx(bank(2 + 2 * h + i, H), T.wq_c[:, KW * i:KW * (i + 1)], T.wq_s[:, KW * i:KW * (i + 1)],
-                         T.xq_c[:, cw], T.xq_s[:, cw], True, True).then_inc(S["zq%d%d" % (i, h)], 1)
-    for h in range(2):
-        cw = slice(H * h, H * h + H)
-        lo, hi = 4 * H * h, 4 * H * (h + 1)
-        act = S["qact%d" % h]
-        V.wait_ge(S["zq0%d" % h], 1)
-        V.tensor_scalar(T.q_t[:, lo + 0:hi:4], bank(2 + 2 * h, H), 0.0, C, MAX, MUL).then_inc(act, 1)
-        V.tensor_scalar(T.q_t[:, lo + 1:hi:4], bank(2 + 2 * h, H), -C, 0.0, MUL, MAX).then_inc(act, 1)
-        A.wait_ge(S["zq1%d" % h], 1)
-        A.activation(T.q_t[:, lo + 2:hi:4], bank(3 + 2 * h, H), RELU, scale=C).then_inc(act, 1)
-        A.activation(T.q_t[:, lo + 3:hi:4], bank(3 + 2 * h, H), RELU, scale=-C).then_inc(act, 1)
-        V.wait_ge(act, 4)
-        V.quantize_mx(T.q_c[:, cw], T.q_s[:, cw], T.q_t[:, lo:hi]).then_inc(S["qq%d" % h], 1)
+            PE.wait_ge(S["qwq%d" % i], 1)
+            wc, ws = wtile(T.wq_c, T.wq_s, i)
+            PE.matmul_mx(bank(2 + 2 * p + i, n), wc, ws, T.xq_c[:, a:a + n], T.xq_s[:, a:a + n],
+                         True, True).then_inc(S["zq%d%d" % (i, p)], 1)
+        A.wait_ge(S["zq1%d" % p], 1)
+        A.activation(T.q_t[:, 4 * a + 2:4 * (a + n):4], bank(3 + 2 * p, n), RELU, scale=C).then_inc(S["qact%d" % p], 1)
+        A.activation(T.q_t[:, 4 * a + 3:4 * (a + n):4], bank(3 + 2 * p, n), RELU, scale=-C).then_inc(S["qact%d" % p], 1)
 
-    def ycols(s, a=0, n=NC):
-        j = src_of[s]
-        return slice(NC * j + a, NC * j + a + n)
-
-    PE.wait_ge(S.kq, 1)
-    PE.wait_ge(S.qq0, 1)
-    PE.matmul_mx(bank(6, H), T.ka_c[:, 0:KW], T.ka_s[:, 0:KW], T.q_c[:, 0:H], T.q_s[:, 0:H], True, True).then_inc(S.my0a, 1)
-    PE.wait_ge(S.qq1, 1)
-    PE.matmul_mx(bank(7, H), T.ka_c[:, 0:KW], T.ka_s[:, 0:KW], T.q_c[:, H:NC], T.q_s[:, H:NC], True, True).then_inc(S.my0b, 1)
-    A.wait_ge(S.my0a, 1)
-    A.activation(T.y_t[:, ycols(0, 0, H)], bank(6, H), COPY).then_inc(S.cp0, 1)
-    V.wait_ge(S.my0b, 1)
-    V.tensor_copy(T.y_t[:, ycols(0, H, H)], bank(7, H)).then_inc(S.cp0, 1)
-    SY.wait_ge(S.cp0, 2)
-    SY.dma_start(T.y[:, ycols(0)], T.y_t[:, ycols(0)]).then_inc(S.st_sy, 16)
-    n_sy, n_sc = 1, 0
-
-    PE.wait_ge(S.kact, 4)
-    PE.wait_ge(S.qact0, 4)
-    PE.wait_ge(S.qact1, 4)
-    order = list(range(1, N))
-    for b, s in enumerate(order):
-        for w in arrive[s]:
+    jobs = [(0, 0, H, 0, "A", [(S.kact, 4)], (0, H, [0])), (1, 0, H, 1, "A", [(S.kact, 4)], (0, H, [1])),
+            (0, H, H, 2, "V", [(S.qact0, 4)], (H, H, [2])), (1, H, H, 3, "V", [(S.qact0, 4)], (H, H, [3])),
+            (2, 0, NC, 4, "A", [(S.qact1, 4)], (0, NC, [4])), (3, 0, NC, 5, "V", [(S.qact1, 4)], (0, NC, [5])),
+            (4, 0, NC, 6, "A", [(S.qact2, 4)], (0, NC, [6])), (5, 0, NC, 7, "V", [(S.qact2, 4)], (0, NC, [7])),
+            (6, 0, NC, 0, "A", [(S.cj0, 1)], (0, NC, [8])),
+            (7, 0, H, 1, "V", [(S.cj1, 1)], None), (7, H, H, 2, "A", [(S.cj2, 1)], (0, NC, [9, 10]))]
+    n_st = {"A": 0, "SY": 0}
+    for u, (s, a, n, b, eng, free, store) in enumerate(jobs):
+        for w in arrive[s] + free:
             PE.wait_ge(*w)
-        if b >= 6:
-            PE.wait_ge(S.cp0, 2)
-        if b == len(order) - 1:
-            for h, sem in enumerate((S.myLa, S.myLb)):
-                PE.matmul_mx(bank(b + h, H), T.ka_c[:, KW * s:KW * (s + 1)], T.ka_s[:, KW * s:KW * (s + 1)],
-                             T.q_c[:, H * h:H * h + H], T.q_s[:, H * h:H * h + H], True, True).then_inc(sem, 1)
-            V.wait_ge(S.myLa, 1)
-            V.tensor_copy(T.y_t[:, ycols(s, 0, H)], bank(b, H)).then_inc(S.cpL, 1)
-            A.wait_ge(S.myLb, 1)
-            A.activation(T.y_t[:, ycols(s, H, H)], bank(b + 1, H), COPY).then_inc(S.cpL, 1)
-            A.wait_ge(S.cpL, 2)
-            A.dma_start(T.y[:, ycols(s)], T.y_t[:, ycols(s)]).then_inc(S.st_sc, 16)
-            n_sc += 1
-            break
-        PE.matmul_mx(bank(b), T.ka_c[:, KW * s:KW * (s + 1)], T.ka_s[:, KW * s:KW * (s + 1)], T.q_c[:], T.q_s[:],
-                     True, True).then_inc(S["my%d" % s], 1)
-        cp = S["cp%d" % s]
-        if b % 2 == 0:
-            A.wait_ge(S["my%d" % s], 1)
-            A.activation(T.y_t[:, ycols(s)], bank(b), COPY).then_inc(cp, 1)
-            A.wait_ge(cp, 1)
-            A.dma_start(T.y[:, ycols(s)], T.y_t[:, ycols(s)]).then_inc(S.st_sc, 16)
-            n_sc += 1
+        for p, (pa, pn) in enumerate(PIECES):
+            if pa < a + n and a < pa + pn:
+                PE.wait_ge(S["qq%d" % p], 1)
+        kc, ks = wtile(T.ka_c, T.ka_s, s)
+        PE.matmul_mx(bank(b, n), kc, ks, T.q_c[:, a:a + n], T.q_s[:, a:a + n], True, True).then_inc(S["mj%d" % u], 1)
+        y0 = NC * src_of[s]
+        if eng == "A":
+            A.wait_ge(S["mj%d" % u], 1)
+            A.activation(T.y_t[:, y0 + a:y0 + a + n], bank(b, n), COPY).then_inc(S["cj%d" % u], 1)
         else:
-            V.wait_ge(S["my%d" % s], 1)
-            V.tensor_copy(T.y_t[:, ycols(s)], bank(b)).then_inc(cp, 1)
-            SY.wait_ge(cp, 1)
-            SY.dma_start(T.y[:, ycols(s)], T.y_t[:, ycols(s)]).then_inc(S.st_sy, 16)
-            n_sy += 1
-    SY.wait_ge(S.st_sy, 16 * n_sy)
-    A.wait_ge(S.st_sc, 16 * n_sc)
+            V.wait_ge(S["mj%d" % u], 1)
+            V.tensor_copy(T.y_t[:, y0 + a:y0 + a + n], bank(b, n)).then_inc(S["cj%d" % u], 1)
+        if store is not None:
+            sa, sn, deps = store
+            Q, sem, key = (A, S.st_sc, "A") if eng == "A" else (SY, S.st_sy, "SY")
+            for d in deps:
+                Q.wait_ge(S["cj%d" % d], 1)
+            Q.dma_start(T.y[:, y0 + sa:y0 + sa + sn], T.y_t[:, y0 + sa:y0 + sa + sn]).then_inc(sem, 16)
+            n_st[key] += 1
+    SY.wait_ge(S.st_sy, 16 * n_st["SY"])
+    A.wait_ge(S.st_sc, 16 * n_st["A"])

from concourse.bass import DstId, RemoteDMATransfer
from concourse.mybir import dt, AluOpType, ActivationFunctionType

N = 8
C = 0.041
KW = 128
NC = 512
H = NC // 2
PIECES = [(0, 256), (256, 128), (384, 128)]
NP = len(PIECES)

SCRATCH = {
    "xk_t": ("sbuf", [128, 4 * KW], "bfloat16"),
    "wk_t": ("sbuf", [128, 8 * KW], "bfloat16"),
    "xq_t": ("sbuf", [128, 4 * NC], "bfloat16"),
    "wq_t": ("sbuf", [128, 8 * KW], "bfloat16"),
    "xk_c": ("sbuf", [128, KW], "float8_e4m3fn_x4"), "xk_s": ("sbuf", [128, KW], "uint8"),
    "wk_c": ("sbuf", [128, 2 * KW], "float8_e4m3fn_x4"), "wk_s": ("sbuf", [128, 2 * KW], "uint8"),
    "xq_c": ("sbuf", [128, NC], "float8_e4m3fn_x4"), "xq_s": ("sbuf", [128, NC], "uint8"),
    "wq_c": ("sbuf", [128, 2 * KW], "float8_e4m3fn_x4"), "wq_s": ("sbuf", [128, 2 * KW], "uint8"),
    "k_t": ("sbuf", [128, 4 * KW], "bfloat16"),
    "q_t": ("sbuf", [128, 4 * NC], "bfloat16"),
    "q_c": ("sbuf", [128, NC], "float8_e4m3fn_x4"), "q_s": ("sbuf", [128, NC], "uint8"),
    "ka_c": ("sbuf", [128, N * KW], "float8_e4m3fn_x4"), "ka_s": ("sbuf", [128, N * KW], "uint8"),
    "ps": ("psum", [128, 8 * 512], "float32"),
    "y_t": ("sbuf", [128, N * NC], "float32"),
}
SEMAPHORES = (["ld_xk", "ld_wk", "ld_wq0", "ld_wq1", "qxk", "qwk0", "qwk1", "zk0", "zk1", "kact", "kq", "qwq0", "qwq1",
               "st_sy", "st_sc", "sent", "fwp"]
              + ["ld_xq%d" % p for p in range(NP)] + ["qxq%d" % p for p in range(NP)]
              + ["zq%d%d" % (i, p) for i in range(2) for p in range(NP)]
              + ["qact%d" % p for p in range(NP)] + ["qq%d" % p for p in range(NP)]
              + ["mj%d" % u for u in range(11)] + ["cj%d" % u for u in range(11)]
              + ["arrp%d" % j for j in range(N)] + ["arrc%d" % j for j in range(N)] + ["fwc%d" % j for j in range(N)]
              + ["hp%d" % j for j in range(N)] + ["hc%d" % j for j in range(N)])


def _count(mask):
    return sum((mask >> b) & 1 for b in range(16))


def rank_program(g, core, T, topo):
    S = T.sem
    V, A, PE, SY = g.vector, g.scalar, g.tensor, g.sync
    MAX, MUL = AluOpType.max, AluOpType.mult
    RELU, COPY = ActivationFunctionType.Relu, ActivationFunctionType.Copy

    cores = list(T.cores)
    chips = []
    for c in cores:
        if topo.chip(c) not in chips:
            chips.append(topo.chip(c))
    members = {ch: [c for c in cores if topo.chip(c) == ch] for ch in chips}
    nch = len(chips)

    def by_helper(ch):
        return [x for x in chips if x != ch and topo.same_plane(ch, x)]

    def by_rank(ch):
        return [x for x in chips if x != ch and not topo.same_plane(ch, x)]

    def send_order(ch):
        return sorted(by_rank(ch), key=lambda x: (chips.index(x) - chips.index(ch)) % nch)

    def recv_order(ch):
        return sorted(by_rank(ch), key=lambda x: (chips.index(ch) - chips.index(x)) % nch)

    nf = len(by_rank(chips[0]))
    hs = 2 + 2 * nf

    def helper_dests(c):
        ch = topo.chip(c)
        p = members[ch].index(c)
        out = []
        for x in by_helper(ch):
            out += [(members[x][p], hs), (members[x][1 - p], hs + 1)]
        return out

    def helper(c):
        ch = topo.chip(c)
        cand = [h for h in range(topo.CHIPS * topo.CORES_PER_CHIP)
                if topo.chip(h) == ch and h not in cores and topo.die(h) != topo.die(c)
                and all(topo.may_write(h, d) for d, _ in helper_dests(c))]
        return cand[members[ch].index(c)]

    def plan(c):
        ch = topo.chip(c)
        p = members[ch].index(c)
        tw = members[ch][1 - p]
        far = [(members[x][p], 2 + recv_order(x).index(ch)) for x in send_order(ch)]
        m_on = topo.mask(c, tw) & topo.mask(c, helper(c))
        m_far = m_on
        for d, _ in far:
            m_far &= topo.mask(c, d)
        m_tw = (m_on & ~m_far) or m_on
        return tw, far, m_far, m_tw, m_on

    def helper_mask(c):
        h = helper(c)
        m = topo.mask(h, c)
        for d, _ in helper_dests(c):
            m &= topo.mask(h, d)
        return m

    def dst_id(c):
        rid, pid, _ = topo.addr(c)
        return DstId(rid=rid, pnc=pid)

    def codes(a, n=1):
        return T.ka_c[:, KW * a:KW * (a + n)].bitcast(dt.uint8)

    def plane(a, n=1):
        return T.ka_s[:, KW * a:KW * (a + n)]

    sent = [0]

    def send(view, a, n, dests, mask, sem):
        g.remote_dma_fused([RemoteDMATransfer(dst_ids=[dst_id(c) for c, _ in dests], dma_engine_mask=mask,
                                              remote_sem=sem, srcs=[view(a, n)], dsts=[view(s, n) for _, s in dests])],
                           local_sem=S.sent)
        sent[0] += _count(mask)

    rank = T.rank_of(core)
    if rank is None:
        for c in cores:
            if helper(c) == core:
                r = T.rank_of(c)
                e = _count(plan(c)[3])
                g.wait_ge(S["arrp%d" % r], e)
                send(plane, 0, 1, helper_dests(c), helper_mask(c), S["hp%d" % r])
                g.wait_ge(S["arrc%d" % r], e)
                send(codes, 0, 1, helper_dests(c), helper_mask(c), S["hc%d" % r])
                g.wait_ge(S.sent, sent[0])
        return

    me = topo.chip(core)
    pos = members[me].index(core)
    twin, far, m_far, m_tw, m_on = plan(core)

    def fwd_mask(c, s):
        return plan(c)[4] if s == 1 + nf else plan(c)[3]

    hx = by_helper(me)[0]
    src_core = ([core, twin] + [members[x][pos] for x in recv_order(me)] + [members[x][1 - pos] for x in recv_order(me)]
                + [members[hx][pos], members[hx][1 - pos]])
    src_of = [T.rank_of(c) for c in src_core]
    e_tw = _count(plan(twin)[3])
    arrive = {0: [(S.kq, 1)], 1: [(S["arrp%d" % src_of[1]], e_tw), (S["arrc%d" % src_of[1]], e_tw)]}
    for s in range(2, 2 + nf):
        e = _count(plan(src_core[s])[2])
        arrive[s] = [(S["arrp%d" % src_of[s]], e), (S["arrc%d" % src_of[s]], e)]
    for s in range(2 + nf, hs):
        arrive[s] = [(S.fwp, e_tw), (S["fwc%d" % s], _count(fwd_mask(twin, s - nf)))]
    for s in range(hs, N):
        e = _count(helper_mask(src_core[s]))
        arrive[s] = [(S["hp%d" % src_of[s]], e), (S["hc%d" % src_of[s]], e)]

    def bank(b, n=NC):
        return T.ps[:, 512 * b:512 * b + n]

    def wtile(c, s, i):
        return c[:, KW * i:KW * (i + 1)], s[:, KW * i:KW * (i + 1)]

    SY.dma_start(T.xk_t[:], T.xk[:]).then_inc(S.ld_xk, 16)
    A.dma_start(T.wk_t[:], T.wk[:]).then_inc(S.ld_wk, 16)
    for i in range(2):
        A.dma_start(T.wq_t[:, 4 * KW * i:4 * KW * (i + 1)], T.wq[:, 4 * KW * i:4 * KW * (i + 1)]).then_inc(S["ld_wq%d" % i], 16)
    for p, (a, n) in enumerate(PIECES):
        SY.dma_start(T.xq_t[:, 4 * a:4 * (a + n)], T.xq[:, 4 * a:4 * (a + n)]).then_inc(S["ld_xq%d" % p], 16)

    V.wait_ge(S.ld_xk, 16)
    V.quantize_mx(T.xk_c[:], T.xk_s[:], T.xk_t[:]).then_inc(S.qxk, 1)
    V.wait_ge(S.ld_wk, 16)
    V.quantize_mx(T.wk_c[:, 0:KW], T.wk_s[:, 0:KW], T.wk_t[:, 0:4 * KW]).then_inc(S.qwk0, 1)
    V.quantize_mx(T.wk_c[:, KW:2 * KW], T.wk_s[:, KW:2 * KW], T.wk_t[:, 4 * KW:8 * KW]).then_inc(S.qwk1, 1)
    PE.wait_ge(S.qxk, 1)
    PE.wait_ge(S.qwk0, 1)
    PE.matmul_mx(bank(0, KW), T.wk_c[:, 0:KW], T.wk_s[:, 0:KW], T.xk_c[:], T.xk_s[:], True, True).then_inc(S.zk0, 1)
    PE.wait_ge(S.qwk1, 1)
    PE.matmul_mx(bank(1, KW), T.wk_c[:, KW:2 * KW], T.wk_s[:, KW:2 * KW], T.xk_c[:], T.xk_s[:], True, True).then_inc(S.zk1, 1)
    A.wait_ge(S.zk0, 1)
    A.activation(T.k_t[:, 0:4 * KW:4], bank(0, KW), RELU, scale=C).then_inc(S.kact, 1)
    A.activation(T.k_t[:, 1:4 * KW:4], bank(0, KW), RELU, scale=-C).then_inc(S.kact, 1)
    V.wait_ge(S.zk1, 1)
    V.tensor_scalar(T.k_t[:, 2:4 * KW:4], bank(1, KW), 0.0, C, MAX, MUL).then_inc(S.kact, 1)
    V.tensor_scalar(T.k_t[:, 3:4 * KW:4], bank(1, KW), -C, 0.0, MUL, MAX).then_inc(S.kact, 1)
    V.wait_ge(S.kact, 4)
    V.quantize_mx(T.ka_c[:, 0:KW], T.ka_s[:, 0:KW], T.k_t[:]).then_inc(S.kq, 1)

    my_p, my_c = S["arrp%d" % rank], S["arrc%d" % rank]
    on_chip = [(helper(core), 0), (twin, 1)]
    g.wait_ge(S.kq, 1)
    send(plane, 0, 1, far, m_far, my_p)
    send(codes, 0, 1, far, m_far, my_c)
    send(plane, 0, 1, on_chip, m_tw, my_p)
    send(codes, 0, 1, on_chip, m_tw, my_c)
    for s in range(2, 2 + nf):
        g.wait_ge(*arrive[s][0])
    send(plane, 2, nf, [(twin, 2 + nf)], m_tw, S.fwp)
    for s in range(2, 2 + nf):
        g.wait_ge(*arrive[s][1])
        send(codes, s, 1, [(twin, s + nf)], fwd_mask(core, s), S["fwc%d" % (s + nf)])
    g.wait_ge(S.sent, sent[0])

    def quant_wq(i):
        V.wait_ge(S["ld_wq%d" % i], 16)
        V.quantize_mx(T.wq_c[:, KW * i:KW * (i + 1)], T.wq_s[:, KW * i:KW * (i + 1)],
                      T.wq_t[:, 4 * KW * i:4 * KW * (i + 1)]).then_inc(S["qwq%d" % i], 1)

    def quant_xq(p):
        a, n = PIECES[p]
        V.wait_ge(S["ld_xq%d" % p], 16)
        V.quantize_mx(T.xq_c[:, a:a + n], T.xq_s[:, a:a + n], T.xq_t[:, 4 * a:4 * (a + n)]).then_inc(S["qxq%d" % p], 1)

    def signs_v(p):
        a, n = PIECES[p]
        V.wait_ge(S["zq0%d" % p], 1)
        V.tensor_scalar(T.q_t[:, 4 * a + 0:4 * (a + n):4], bank(2 + 2 * p, n), 0.0, C, MAX, MUL).then_inc(S["qact%d" % p], 1)
        V.tensor_scalar(T.q_t[:, 4 * a + 1:4 * (a + n):4], bank(2 + 2 * p, n), -C, 0.0, MUL, MAX).then_inc(S["qact%d" % p], 1)

    def quant_q(p):
        a, n = PIECES[p]
        V.wait_ge(S["qact%d" % p], 4)
        V.quantize_mx(T.q_c[:, a:a + n], T.q_s[:, a:a + n], T.q_t[:, 4 * a:4 * (a + n)]).then_inc(S["qq%d" % p], 1)

    quant_wq(0)
    quant_xq(0)
    quant_wq(1)
    quant_xq(1)
    signs_v(0)
    quant_xq(2)
    quant_q(0)
    signs_v(1)
    quant_q(1)
    signs_v(2)
    quant_q(2)
    for p, (a, n) in enumerate(PIECES):
        PE.wait_ge(S["qxq%d" % p], 1)
        for i in range(2):
            PE.wait_ge(S["qwq%d" % i], 1)
            wc, ws = wtile(T.wq_c, T.wq_s, i)
            PE.matmul_mx(bank(2 + 2 * p + i, n), wc, ws, T.xq_c[:, a:a + n], T.xq_s[:, a:a + n],
                         True, True).then_inc(S["zq%d%d" % (i, p)], 1)
        A.wait_ge(S["zq1%d" % p], 1)
        A.activation(T.q_t[:, 4 * a + 2:4 * (a + n):4], bank(3 + 2 * p, n), RELU, scale=C).then_inc(S["qact%d" % p], 1)
        A.activation(T.q_t[:, 4 * a + 3:4 * (a + n):4], bank(3 + 2 * p, n), RELU, scale=-C).then_inc(S["qact%d" % p], 1)

    jobs = [(0, 0, H, 0, "A", [(S.kact, 4)], (0, H, [0])), (1, 0, H, 1, "A", [(S.kact, 4)], (0, H, [1])),
            (0, H, H, 2, "V", [(S.qact0, 4)], (H, H, [2])), (1, H, H, 3, "V", [(S.qact0, 4)], (H, H, [3])),
            (2, 0, NC, 4, "A", [(S.qact1, 4)], (0, NC, [4])), (3, 0, NC, 5, "V", [(S.qact1, 4)], (0, NC, [5])),
            (4, 0, NC, 6, "A", [(S.qact2, 4)], (0, NC, [6])), (5, 0, NC, 7, "V", [(S.qact2, 4)], (0, NC, [7])),
            (6, 0, NC, 0, "A", [(S.cj0, 1)], (0, NC, [8])),
            (7, 0, H, 1, "V", [(S.cj1, 1)], None), (7, H, H, 2, "A", [(S.cj2, 1)], (0, NC, [9, 10]))]
    n_st = {"A": 0, "SY": 0}
    for u, (s, a, n, b, eng, free, store) in enumerate(jobs):
        for w in arrive[s] + free:
            PE.wait_ge(*w)
        for p, (pa, pn) in enumerate(PIECES):
            if pa < a + n and a < pa + pn:
                PE.wait_ge(S["qq%d" % p], 1)
        kc, ks = wtile(T.ka_c, T.ka_s, s)
        PE.matmul_mx(bank(b, n), kc, ks, T.q_c[:, a:a + n], T.q_s[:, a:a + n], True, True).then_inc(S["mj%d" % u], 1)
        y0 = NC * src_of[s]
        if eng == "A":
            A.wait_ge(S["mj%d" % u], 1)
            A.activation(T.y_t[:, y0 + a:y0 + a + n], bank(b, n), COPY).then_inc(S["cj%d" % u], 1)
        else:
            V.wait_ge(S["mj%d" % u], 1)
            V.tensor_copy(T.y_t[:, y0 + a:y0 + a + n], bank(b, n)).then_inc(S["cj%d" % u], 1)
        if store is not None:
            sa, sn, deps = store
            Q, sem, key = (A, S.st_sc, "A") if eng == "A" else (SY, S.st_sy, "SY")
            for d in deps:
                Q.wait_ge(S["cj%d" % d], 1)
            Q.dma_start(T.y[:, y0 + sa:y0 + sa + sn], T.y_t[:, y0 + sa:y0 + sa + sn]).then_inc(sem, 16)
            n_st[key] += 1
    SY.wait_ge(S.st_sy, 16 * n_st["SY"])
    A.wait_ge(S.st_sc, 16 * n_st["A"])
